import numpy as np
import ml_dtypes


def mxq(x, axis, fmt="e4m3"):
    dtype, down = {"e4m3": (ml_dtypes.float8_e4m3fn, 7), "e5m2": (ml_dtypes.float8_e5m2, 14)}[fmt]
    v = np.moveaxis(np.asarray(x, np.float32).astype(ml_dtypes.bfloat16).astype(np.float64), axis, -1)
    blocks = v.reshape(v.shape[:-1] + (-1, 32))
    amax = np.abs(blocks).max(-1, keepdims=True)
    byte = np.maximum(np.where(amax > 0, np.frexp(amax)[1] - 1 + 127, 0) - down, 1)
    scale = np.exp2(byte - 127.0)
    codes = (blocks / scale).astype(np.float32).astype(dtype).astype(np.float64)
    return np.moveaxis((codes * scale).reshape(v.shape), -1, axis)


WIDE = False


def mx_kscale(k):
    if not WIDE:
        return np.ones(k)
    levels = np.array([10, -10, 5, -5, 0])
    if k % 512:
        return np.exp2(np.random.permutation(np.resize(levels, k // 32))).repeat(32)
    a = np.empty((k // 512, 16))
    for p in range(k // 512):
        a[p, :8] = np.random.permutation(np.resize(levels, 8))
        for g in range(8):
            far = levels[np.abs(levels - a[p, g]) >= 10]
            a[p, g + 8] = far[np.random.randint(len(far))]
    return np.exp2(a.ravel()).repeat(32)


def f64(x):
    return np.asarray(x).astype(np.float64)


def striped(idx):
    return np.tile(np.asarray(idx).reshape(-1, 16).T, (8, 1)).astype(np.uint16)


def unstriped(offs):
    return offs[:16].T.reshape(-1).astype(np.int64)


def striped8(idx):
    return np.asarray(idx).reshape(8, -1, 16).transpose(0, 2, 1).reshape(128, -1).astype(np.uint16)


def unstriped8(offs):
    return offs.reshape(8, 16, -1).transpose(0, 2, 1).reshape(8, -1).astype(np.int64)


def pick8(x, idx, run):
    r = np.arange(len(x))
    return x[r[:, None], idx[r % (8 * run) // run]]


E2M1 = np.array([0.0, 0.5, 1.0, 1.5, 2.0, 3.0, 4.0, 6.0, -0.0, -0.5, -1.0, -1.5, -2.0, -3.0, -4.0, -6.0])


def pack_weight(w, fmt):
    k, n = w.shape
    w = f64(np.asarray(w, np.float32).astype(ml_dtypes.bfloat16)).reshape(k // 32, 32, n)
    amax = np.abs(w).max(1)
    if fmt == "e4m3":
        byte = np.frexp(amax)[1] - 1 + 127 - 7
    else:
        mant, ex = np.frexp(amax / 6.0)
        byte = np.where(mant > 0.5, ex, ex - 1) + 127
    byte = np.clip(np.where(amax > 0, byte, 1), 1, 254)
    scaled = (w * np.exp2(127.0 - byte)[:, None, :]).reshape(k, n).astype(np.float32)
    by_word = np.ascontiguousarray(scaled.reshape(k // 512, 128, 4, n).transpose(0, 1, 3, 2))
    if fmt == "e4m3":
        words = by_word.astype(ml_dtypes.float8_e4m3fn).view(np.uint8)
    else:
        c = by_word.astype(ml_dtypes.float4_e2m1fn).view(np.uint8) & 0xF
        words = (c[..., 0::2] | (c[..., 1::2] << 4)).reshape(k // 512, 128, 2 * n)
    return np.ascontiguousarray(words), np.ascontiguousarray(byte.astype(np.uint8).reshape(k // 512, 16, n))


def unpack_weight(words, scales, fmt):
    g, _, n = scales.shape
    words = np.ascontiguousarray(words).reshape(g, 128, n, -1)
    if fmt == "e4m3":
        vals = words.view(ml_dtypes.float8_e4m3fn).astype(np.float64)
    else:
        nib = np.empty((g, 128, n, 4), np.uint8)
        nib[..., 0::2] = words & 0xF
        nib[..., 1::2] = words >> 4
        vals = E2M1[nib]
    vals = vals * np.repeat(np.exp2(scales.astype(np.float64) - 127.0), 8, axis=1)[..., None]
    return vals.transpose(0, 1, 3, 2).reshape(g * 512, n)


K, J, R, T, F, O, S, C, N = 512, 512, 512, 1024, 1024, 256, 256, 512, 256


def setup_inputs():
    n = np.random.standard_normal
    idx = np.random.permutation(T)[:J]
    idx2 = np.random.permutation(F)[:R]
    idx3 = np.stack([np.random.permutation(J)[:S] for _ in range(8)])
    idx4 = np.stack([np.random.permutation(J)[:S] for _ in range(8)])
    idx5 = np.stack([np.random.permutation(C)[:S] for _ in range(8)])
    idx6 = np.stack([np.random.permutation(C)[:S] for _ in range(8)])
    idx7 = np.stack([np.random.permutation(C)[:O] for _ in range(8)])
    fk = mx_kscale(K)
    fr = mx_kscale(R)
    tr = np.ones(F)
    tr[idx2] = fr
    xtp = pack_weight(n((K, T)) * fk[:, None], "e4m3")
    wtp = pack_weight(n((K, F)) * 1 / np.sqrt(K) / fk[:, None] * tr, "e2m1")
    wbp = pack_weight(n((R, N)) * 1 / np.sqrt(R) / fr[:, None], "e4m3")
    return {
        "xt_words": xtp[0],
        "xt_scales": xtp[1],
        "wt_words": wtp[0],
        "wt_scales": wtp[1],
        "sa": (np.random.uniform(0.5, 1.6, (R, 1))).astype(np.float32),
        "sb": (np.random.uniform(0.5, 1.6, (R, 1))).astype(np.float32),
        "sd": (np.random.uniform(0.5, 1.6, (R, 1))).astype(np.float32),
        "wb_words": wbp[0],
        "wb_scales": wbp[1],
        "offs": striped(idx),
        "offs2": striped(idx2),
        "offs3": striped8(idx3),
        "offs4": striped8(idx4),
        "offs5": striped8(idx5),
        "offs6": striped8(idx6),
        "offs7": striped8(idx7),
    }


def reference(xt_words, xt_scales, wt_words, wt_scales, sa, sb, sd, wb_words, wb_scales, offs, offs2, offs3, offs4, offs5, offs6, offs7):
    idx = unstriped(offs)
    idx2 = unstriped(offs2)
    idx3 = unstriped8(offs3)
    idx4 = unstriped8(offs4)
    idx5 = unstriped8(offs5)
    idx6 = unstriped8(offs6)
    idx7 = unstriped8(offs7)
    xtu = unpack_weight(xt_words, xt_scales, "e4m3")
    wtu = unpack_weight(wt_words, wt_scales, "e2m1")
    wbu = unpack_weight(wb_words, wb_scales, "e4m3")
    wtidx2g = wtu[:, idx2]
    xtidxg = xtu[:, idx]
    a = wtidx2g.T @ xtidxg
    h1 = pick8(a, idx3, 64) * f64(sa)
    h2 = pick8(a, idx4, 64) * f64(sb)
    pw = np.zeros((R, C))
    pw[np.arange(R)[:, None], idx5[np.arange(R) % 512 // 64]] = h1
    pv = np.zeros((R, C))
    pv[np.arange(R)[:, None], idx6[np.arange(R) % 512 // 64]] = h2
    g1 = np.abs(pw - pv)
    hid = pick8(g1, idx7, 64) * f64(sd)
    hidq = mxq(hid, 0, "e4m3")
    y = wbu.T @ hidq
    return y

@@ -1,0 +1,188 @@
+from contextlib import ExitStack
+
+import concourse.mybir as mybir
+
+K, J, R, T, F, O, S, C, N = 512, 512, 512, 1024, 1024, 256, 256, 512, 256
+FLOPS = 2 * K * R * J + 2 * R * N * O
+
+F32 = mybir.dt.float32
+BF16 = mybir.dt.bfloat16
+I32 = mybir.dt.int32
+U32 = mybir.dt.uint32
+U16 = mybir.dt.uint16
+U8 = mybir.dt.uint8
+FP8X4 = mybir.dt.float8_e4m3fn_x4
+FP4X4 = mybir.dt.float4_e2m1fn_x4
+ALU = mybir.AluOpType
+COPY = mybir.ActivationFunctionType.Copy
+
+P = 128
+PACK = 4
+HALF = O // 2
+SLOT_PIECES = ((0, 256), (256, 384), (384, 512))
+
+
+def load_scale_rows(nc, plane, rows):
+    for q in range(4):
+        nc.sync.dma_start(out=plane[32 * q : 32 * q + 4, :].bitcast(I32), in_=rows[4 * q : 4 * q + 4, :].bitcast(I32))
+
+
+def tile_picked_tokens_store_one_doublepost_one_plain_kernel(
+    tc, xt_words, xt_scales, wt_words, wt_scales, sa, sb, sd, wb_words, wb_scales,
+    offs, offs2, offs3, offs4, offs5, offs6, offs7, out,
+):
+    nc = tc.nc
+    with ExitStack() as ctx:
+        keep = ctx.enter_context(tc.tile_pool(name="keep", bufs=1))
+        psum = ctx.enter_context(tc.psum_pool(name="psum", bufs=1))
+
+        def sb_tile(name, shape, dtype, tag=None):
+            return keep.tile(shape, dtype, name=name, tag=tag or name, align_bytes=64)
+
+        def load_list(name, src):
+            lst = keep.tile(list(src.shape), U16, name=name)
+            nc.sync.dma_start(lst[:], src)
+            return lst
+
+        def load_row_weights(name, src):
+            w = keep.tile([P, PACK], F32, name=name)
+            nc.sync.dma_start(out=w[:], in_=src.rearrange("(p t) one -> p (t one)", t=PACK))
+            return w
+
+        wt_scale_table = sb_tile("wt_scale_table", [P, F], U8)
+        xt_scale_table = sb_tile("xt_scale_table", [P, T], U8)
+        wb_scale = sb_tile("wb_scale", [P, N], U8)
+        for plane in (wt_scale_table, xt_scale_table, wb_scale):
+            nc.vector.memset(plane[:].bitcast(I32), 0)
+        boards_w = [sb_tile("board_w%d" % i, [P, C], F32) for i in range(2)]
+        boards_v = [sb_tile("board_v%d" % i, [P, C], F32) for i in range(2)]
+        for i in range(2):
+            nc.vector.memset(boards_w[i][:], 0.0)
+            nc.vector.memset(boards_v[i][:], 0.0)
+
+        feature_list = load_list("feature_list", offs2)
+        wt_word_table = sb_tile("wt_word_table", [P, F], U16)
+        nc.sync.dma_start(out=wt_word_table[:].bitcast(I32), in_=wt_words[0].bitcast(I32))
+        load_scale_rows(nc, wt_scale_table, wt_scales[0])
+        token_list = load_list("token_list", offs)
+        xt_word_table = sb_tile("xt_word_table", [P, T], U32)
+        nc.sync.dma_start(
+            out=xt_word_table[:].bitcast(I32), in_=xt_words[0].rearrange("p n t -> p (n t)").bitcast(I32)
+        )
+        load_scale_rows(nc, xt_scale_table, xt_scales[0])
+        first_slots = load_list("first_slots", offs3)
+        first_w = load_row_weights("first_w", sa)
+        second_slots = load_list("second_slots", offs4)
+        second_w = load_row_weights("second_w", sb)
+        first_cols = load_list("first_cols", offs5)
+        second_cols = load_list("second_cols", offs6)
+        place_cols = load_list("place_cols", offs7)
+        read_w = load_row_weights("read_w", sd)
+        wb_word = sb_tile("wb_word", [P, N], U32)
+        nc.sync.dma_start(out=wb_word[:].bitcast(I32), in_=wb_words[0].rearrange("p n t -> p (n t)").bitcast(I32))
+        load_scale_rows(nc, wb_scale, wb_scales[0])
+
+        wt_word = sb_tile("wt_word", [P, R], U16)
+        nc.vector.tensor_copy(wt_word[:], wt_word_table[:].indirect(feature_list[:]))
+        wt_scale = sb_tile("wt_scale", [P, R], U8)
+        nc.vector.tensor_copy(wt_scale[:], wt_scale_table[:].indirect(feature_list[:]))
+
+        word_by_t = wt_word[:].bitcast(U8).rearrange("p (m t b) -> p t m b", t=PACK, b=2)
+        scale_by_t = wt_scale[:].rearrange("p (m t) -> p t m", t=PACK)
+        dealt_word = [None] * PACK
+        dealt_scale = [None] * PACK
+
+        def deal(t0, t1):
+            words = sb_tile("dealt_word%d" % t0, [P, t1 - t0, P, 2], U8)
+            scales = sb_tile("dealt_scale%d" % t0, [P, t1 - t0, P], U8)
+            nc.vector.tensor_copy(words[:], word_by_t[:, t0:t1])
+            nc.vector.tensor_copy(scales[:], scale_by_t[:, t0:t1])
+            for t in range(t0, t1):
+                dealt_word[t] = words[:, t - t0].rearrange("p m b -> p (m b)").bitcast(FP4X4)
+                dealt_scale[t] = scales[:, t - t0]
+
+        deal(0, 1)
+        xt_word = sb_tile("xt_word", [P, J], U32)
+        nc.vector.tensor_copy(xt_word[:], xt_word_table[:].indirect(token_list[:]))
+        xt_scale = sb_tile("xt_scale", [P, J], U8)
+        for j0, j1 in SLOT_PIECES:
+            nc.vector.tensor_copy(xt_scale[:, j0:j1], xt_scale_table[:].indirect(token_list[:, j0 // 16 : j1 // 16]))
+
+        def first_product(t, j0, j1, bank):
+            acc = psum.tile([P, j1 - j0], F32, name="acc_a%d_%d" % (t, j0), tag="bank%d" % bank)
+            nc.tensor.matmul_mx(
+                out=acc[:], lhsT=dealt_word[t], lhsT_scale=dealt_scale[t],
+                rhs=xt_word[:, j0:j1].bitcast(FP8X4), rhs_scale=xt_scale[:, j0:j1], start=True, stop=True,
+            )
+            return acc
+
+        hidden = [sb_tile("hidden%d" % t, [P, J], F32) for t in range(PACK)]
+        for i, (j0, j1) in enumerate(SLOT_PIECES):
+            nc.scalar.activation(hidden[0][:, j0:j1], first_product(0, j0, j1, i)[:], COPY)
+        deal(1, PACK)
+        for t in range(1, PACK):
+            nc.vector.tensor_copy(hidden[t][:], first_product(t, 0, J, 2 + t)[:])
+
+        gaps = []
+        for t in range(PACK):
+            h1 = sb_tile("h1_%d" % t, [P, S], F32)
+            h2 = sb_tile("h2_%d" % t, [P, S], F32)
+            nc.scalar.activation(h1[:], hidden[t][:].indirect(first_slots[:]), COPY, scale=first_w[:, t : t + 1])
+            nc.scalar.activation(h2[:], hidden[t][:].indirect(second_slots[:]), COPY, scale=second_w[:, t : t + 1])
+            board_w, board_v = boards_w[t % 2], boards_v[t % 2]
+            nc.scalar.activation(board_w[:].indirect(first_cols[:]), h1[:], COPY)
+            nc.scalar.activation(board_v[:].indirect(second_cols[:]), h2[:], COPY)
+            diff = sb_tile("diff%d" % t, [P, C], F32)
+            gap = sb_tile("gap%d" % t, [P, C], F32)
+            halves = (slice(0, C // 2), slice(C // 2, C))
+            for cols in halves:
+                nc.vector.tensor_tensor(diff[:, cols], board_w[:, cols], board_v[:, cols], ALU.subtract)
+            for cols in halves:
+                nc.vector.scalar_tensor_tensor(gap[:, cols], diff[:, cols], -1.0, diff[:, cols], ALU.mult, ALU.max)
+            gaps.append(gap)
+
+        planes = [
+            sb_tile("hid_planes0", [P, PACK, HALF], BF16, tag="h2_%d" % (PACK - 1)),
+            sb_tile("hid_planes1", [P, PACK, HALF], BF16, tag="h1_%d" % (PACK - 1)),
+        ]
+        for u in range(2):
+            cols = place_cols[:, u * HALF // 16 : (u + 1) * HALF // 16]
+            for t in range(PACK):
+                nc.scalar.activation(planes[u][:, t], gaps[t][:].indirect(cols), COPY, scale=read_w[:, t : t + 1])
+
+        woven = [sb_tile("woven%d" % u, [P, HALF, PACK], BF16) for u in range(2)]
+        codes = [sb_tile("codes%d" % u, [P, HALF], U32) for u in range(2)]
+        scales = [sb_tile("scales%d" % u, [P, HALF], U8) for u in range(2)]
+        for u in range(2):
+            nc.vector.tensor_copy(
+                woven[u][:].rearrange("p (c i) t -> p c t i", i=4),
+                planes[u][:].rearrange("p t (c i) -> p c t i", i=4),
+            )
+        for u in range(2):
+            nc.vector.quantize_mx(
+                out=codes[u][:].bitcast(FP8X4), scales=scales[u][:], in_=woven[u][:].rearrange("p o t -> p (o t)")
+            )
+
+        def second_product(acc, u, b):
+            nc.tensor.matmul_mx(
+                out=acc, lhsT=wb_word[:, b * P : (b + 1) * P].bitcast(FP8X4), lhsT_scale=wb_scale[:, b * P : (b + 1) * P],
+                rhs=codes[u][:].bitcast(FP8X4), rhs_scale=scales[u][:], start=True, stop=True,
+            )
+
+        out_rows = out.rearrange("(b p) o -> p b o", p=P)
+        acc0 = psum.tile([P, 2, HALF], F32, name="acc_out0", tag="bank0")
+        for b in range(2):
+            second_product(acc0[:, b], 0, b)
+        result0 = sb_tile("result0", [P, 2, HALF], F32)
+        nc.scalar.activation(result0[:], acc0[:], COPY)
+        nc.sync.dma_start(out=out_rows[:, :, 0:HALF], in_=result0[:])
+        for b in range(2):
+            acc = psum.tile([P, HALF], F32, name="acc_out1_%d" % b, tag="bank%d" % (1 + b))
+            second_product(acc[:], 1, b)
+            result = sb_tile("result1_%d" % b, [P, HALF], F32)
+            if b == 0:
+                nc.vector.tensor_copy(result[:], acc[:])
+                nc.sync.dma_start(out=out_rows[:, b, HALF:O], in_=result[:])
+            else:
+                nc.scalar.activation(result[:], acc[:], COPY)
+                nc.scalar.dma_start(out=out_rows[:, b, HALF:O], in_=result[:])

@@ -19,12 +19,12 @@ COPY = mybir.ActivationFunctionType.Copy
 P = 128
 PACK = 4
 HALF = O // 2
-SLOT_PIECES = ((0, 256), (256, 384), (384, 512))
+SLOT_PIECES = ((0, 128), (128, 256), (256, 384), (384, 512))
 
 
-def load_scale_rows(nc, plane, rows):
-    for q in range(4):
-        nc.sync.dma_start(out=plane[32 * q : 32 * q + 4, :].bitcast(I32), in_=rows[4 * q : 4 * q + 4, :].bitcast(I32))
+def load_scale_rows(nc, plane, rows, queues):
+    for q, queue in enumerate(queues):
+        queue.dma_start(out=plane[32 * q : 32 * q + 4, :].bitcast(I32), in_=rows[4 * q : 4 * q + 4, :].bitcast(I32))
 
 
 def tile_picked_tokens_store_one_doublepost_one_plain_kernel(
@@ -34,6 +34,9 @@ def tile_picked_tokens_store_one_doublepost_one_plain_kernel(
     nc = tc.nc
     with ExitStack() as ctx:
         keep = ctx.enter_context(tc.tile_pool(name="keep", bufs=1))
+        reuse = ctx.enter_context(tc.tile_pool(name="reuse", bufs=1))
+        seats = ctx.enter_context(tc.tile_pool(name="seats", bufs=1))
+        picked = ctx.enter_context(tc.tile_pool(name="picked", bufs=1))
         psum = ctx.enter_context(tc.psum_pool(name="psum", bufs=1))
 
         def sb_tile(name, shape, dtype, tag=None):
@@ -49,8 +52,8 @@ def tile_picked_tokens_store_one_doublepost_one_plain_kernel(
             nc.sync.dma_start(out=w[:], in_=src.rearrange("(p t) one -> p (t one)", t=PACK))
             return w
 
-        wt_scale_table = sb_tile("wt_scale_table", [P, F], U8)
-        xt_scale_table = sb_tile("xt_scale_table", [P, T], U8)
+        wt_scale_table = picked.tile([P, F], U8, name="wt_scale_table", offset=0, align_bytes=64)
+        xt_scale_table = reuse.tile([P, T], U8, name="xt_scale_table", offset=0, align_bytes=64)
         wb_scale = sb_tile("wb_scale", [P, N], U8)
         for plane in (wt_scale_table, xt_scale_table, wb_scale):
             nc.vector.memset(plane[:].bitcast(I32), 0)
@@ -63,13 +66,13 @@ def tile_picked_tokens_store_one_doublepost_one_plain_kernel(
         feature_list = load_list("feature_list", offs2)
         wt_word_table = sb_tile("wt_word_table", [P, F], U16)
         nc.sync.dma_start(out=wt_word_table[:].bitcast(I32), in_=wt_words[0].bitcast(I32))
-        load_scale_rows(nc, wt_scale_table, wt_scales[0])
+        load_scale_rows(nc, wt_scale_table, wt_scales[0], [nc.sync] * 4)
         token_list = load_list("token_list", offs)
         xt_word_table = sb_tile("xt_word_table", [P, T], U32)
         nc.sync.dma_start(
             out=xt_word_table[:].bitcast(I32), in_=xt_words[0].rearrange("p n t -> p (n t)").bitcast(I32)
         )
-        load_scale_rows(nc, xt_scale_table, xt_scales[0])
+        load_scale_rows(nc, xt_scale_table, xt_scales[0], [nc.sync] * 4)
         first_slots = load_list("first_slots", offs3)
         first_w = load_row_weights("first_w", sa)
         second_slots = load_list("second_slots", offs4)
@@ -80,33 +83,36 @@ def tile_picked_tokens_store_one_doublepost_one_plain_kernel(
         read_w = load_row_weights("read_w", sd)
         wb_word = sb_tile("wb_word", [P, N], U32)
         nc.sync.dma_start(out=wb_word[:].bitcast(I32), in_=wb_words[0].rearrange("p n t -> p (n t)").bitcast(I32))
-        load_scale_rows(nc, wb_scale, wb_scales[0])
+        load_scale_rows(nc, wb_scale, wb_scales[0], [nc.sync] * 4)
 
         wt_word = sb_tile("wt_word", [P, R], U16)
         nc.vector.tensor_copy(wt_word[:], wt_word_table[:].indirect(feature_list[:]))
         wt_scale = sb_tile("wt_scale", [P, R], U8)
         nc.vector.tensor_copy(wt_scale[:], wt_scale_table[:].indirect(feature_list[:]))
+        xt_word = picked.tile([P, J], U32, name="xt_word", offset=J + 2 * P, align_bytes=64)
+        nc.vector.tensor_copy(xt_word[:], xt_word_table[:].indirect(token_list[:]))
 
-        word_by_t = wt_word[:].bitcast(U8).rearrange("p (m t b) -> p t m b", t=PACK, b=2)
+        word_by_t = wt_word[:].rearrange("p (m t) -> p t m", t=PACK)
         scale_by_t = wt_scale[:].rearrange("p (m t) -> p t m", t=PACK)
         dealt_word = [None] * PACK
         dealt_scale = [None] * PACK
 
-        def deal(t0, t1):
-            words = sb_tile("dealt_word%d" % t0, [P, t1 - t0, P, 2], U8)
-            scales = sb_tile("dealt_scale%d" % t0, [P, t1 - t0, P], U8)
+        def deal(t0, t1, words, scales):
             nc.vector.tensor_copy(words[:], word_by_t[:, t0:t1])
             nc.vector.tensor_copy(scales[:], scale_by_t[:, t0:t1])
             for t in range(t0, t1):
-                dealt_word[t] = words[:, t - t0].rearrange("p m b -> p (m b)").bitcast(FP4X4)
+                dealt_word[t] = words[:, t - t0].bitcast(FP4X4)
                 dealt_scale[t] = scales[:, t - t0]
 
-        deal(0, 1)
-        xt_word = sb_tile("xt_word", [P, J], U32)
-        nc.vector.tensor_copy(xt_word[:], xt_word_table[:].indirect(token_list[:]))
-        xt_scale = sb_tile("xt_scale", [P, J], U8)
+        xt_scale = picked.tile([P, J], U8, name="xt_scale", offset=0, align_bytes=64)
+        deal(
+            0, 1,
+            picked.tile([P, 1, P], U16, name="first_words", offset=J, align_bytes=64),
+            sb_tile("first_scales", [P, 1, P], U8),
+        )
         for j0, j1 in SLOT_PIECES:
-            nc.vector.tensor_copy(xt_scale[:, j0:j1], xt_scale_table[:].indirect(token_list[:, j0 // 16 : j1 // 16]))
+            tokens = token_list[:, j0 // 16 : j1 // 16]
+            nc.vector.tensor_copy(xt_scale[:, j0:j1], xt_scale_table[:].indirect(tokens))
 
         def first_product(t, j0, j1, bank):
             acc = psum.tile([P, j1 - j0], F32, name="acc_a%d_%d" % (t, j0), tag="bank%d" % bank)
@@ -119,49 +125,56 @@ def tile_picked_tokens_store_one_doublepost_one_plain_kernel(
         hidden = [sb_tile("hidden%d" % t, [P, J], F32) for t in range(PACK)]
         for i, (j0, j1) in enumerate(SLOT_PIECES):
             nc.scalar.activation(hidden[0][:, j0:j1], first_product(0, j0, j1, i)[:], COPY)
-        deal(1, PACK)
+        deal(
+            1, PACK,
+            reuse.tile([P, PACK - 1, P], U16, name="later_words", offset=0, align_bytes=64),
+            reuse.tile([P, PACK - 1, P], U8, name="later_scales", offset=2 * (PACK - 1) * P, align_bytes=64),
+        )
         for t in range(1, PACK):
-            nc.vector.tensor_copy(hidden[t][:], first_product(t, 0, J, 2 + t)[:])
+            nc.vector.tensor_copy(hidden[t][:], first_product(t, 0, J, 3 + t)[:])
 
         gaps = []
         for t in range(PACK):
-            h1 = sb_tile("h1_%d" % t, [P, S], F32)
-            h2 = sb_tile("h2_%d" % t, [P, S], F32)
+            h1 = sb_tile("h1_%d" % t, [P, S], F32, tag="h1")
+            h2 = seats.tile([P, S], F32, name="h2_%d" % t, offset=512, align_bytes=64)
             nc.scalar.activation(h1[:], hidden[t][:].indirect(first_slots[:]), COPY, scale=first_w[:, t : t + 1])
             nc.scalar.activation(h2[:], hidden[t][:].indirect(second_slots[:]), COPY, scale=second_w[:, t : t + 1])
             board_w, board_v = boards_w[t % 2], boards_v[t % 2]
             nc.scalar.activation(board_w[:].indirect(first_cols[:]), h1[:], COPY)
             nc.scalar.activation(board_v[:].indirect(second_cols[:]), h2[:], COPY)
-            diff = sb_tile("diff%d" % t, [P, C], F32)
+            diffs = [sb_tile("diff%d_%d" % (t, i), [P, C // 2], F32)[:] for i in range(2)]
+            if t == PACK - 1:
+                late_planes = seats.tile([P, PACK * C], BF16, name="late_planes", offset=1024, align_bytes=64)
+                diffs[1] = late_planes[:, 2 * C : 3 * C].bitcast(F32)
             gap = sb_tile("gap%d" % t, [P, C], F32)
             halves = (slice(0, C // 2), slice(C // 2, C))
-            for cols in halves:
-                nc.vector.tensor_tensor(diff[:, cols], board_w[:, cols], board_v[:, cols], ALU.subtract)
-            for cols in halves:
-                nc.vector.scalar_tensor_tensor(gap[:, cols], diff[:, cols], -1.0, diff[:, cols], ALU.mult, ALU.max)
+            for diff, cols in zip(diffs, halves):
+                nc.vector.tensor_tensor(diff, board_w[:, cols], board_v[:, cols], ALU.subtract)
+            for diff, cols in zip(diffs, halves):
+                nc.vector.scalar_tensor_tensor(gap[:, cols], diff, -1.0, diff, ALU.mult, ALU.max)
             gaps.append(gap)
 
-        planes = [
-            sb_tile("hid_planes0", [P, PACK, HALF], BF16, tag="h2_%d" % (PACK - 1)),
-            sb_tile("hid_planes1", [P, PACK, HALF], BF16, tag="h1_%d" % (PACK - 1)),
-        ]
+        early_planes = seats.tile([P, PACK, HALF], BF16, name="early_planes", offset=0, align_bytes=64)
+        planes = [early_planes[:], late_planes[:].rearrange("p (t x) -> p t x", t=PACK)[:, :, 0:HALF]]
         for u in range(2):
             cols = place_cols[:, u * HALF // 16 : (u + 1) * HALF // 16]
             for t in range(PACK):
                 nc.scalar.activation(planes[u][:, t], gaps[t][:].indirect(cols), COPY, scale=read_w[:, t : t + 1])
 
-        woven = [sb_tile("woven%d" % u, [P, HALF, PACK], BF16) for u in range(2)]
         codes = [sb_tile("codes%d" % u, [P, HALF], U32) for u in range(2)]
         scales = [sb_tile("scales%d" % u, [P, HALF], U8) for u in range(2)]
-        for u in range(2):
-            nc.vector.tensor_copy(
-                woven[u][:].rearrange("p (c i) t -> p c t i", i=4),
-                planes[u][:].rearrange("p t (c i) -> p c t i", i=4),
-            )
-        for u in range(2):
-            nc.vector.quantize_mx(
-                out=codes[u][:].bitcast(FP8X4), scales=scales[u][:], in_=woven[u][:].rearrange("p o t -> p (o t)")
-            )
+        for u, pieces in enumerate((((0, HALF),), ((0, HALF // 2), (HALF // 2, HALF)))):
+            woven = [sb_tile("woven%d_%d" % (u, o0), [P, o1 - o0, PACK], BF16) for o0, o1 in pieces]
+            for tile, (o0, o1) in zip(woven, pieces):
+                nc.vector.tensor_copy(
+                    tile[:].rearrange("p (c i) t -> p c t i", i=4),
+                    planes[u][:, :, o0:o1].rearrange("p t (c i) -> p c t i", i=4),
+                )
+            for tile, (o0, o1) in zip(woven, pieces):
+                nc.vector.quantize_mx(
+                    out=codes[u][:, o0:o1].bitcast(FP8X4), scales=scales[u][:, o0:o1],
+                    in_=tile[:].rearrange("p o t -> p (o t)"),
+                )
 
         def second_product(acc, u, b):
             nc.tensor.matmul_mx(

@@ -63,9 +63,9 @@ def tile_picked_tokens_store_one_doublepost_one_plain_kernel(
             nc.vector.memset(boards_w[i][:], 0.0)
             nc.vector.memset(boards_v[i][:], 0.0)
 
-        feature_list = load_list("feature_list", offs2)
         wt_word_table = sb_tile("wt_word_table", [P, F], U16)
         nc.sync.dma_start(out=wt_word_table[:].bitcast(I32), in_=wt_words[0].bitcast(I32))
+        feature_list = load_list("feature_list", offs2)
         load_scale_rows(nc, wt_scale_table, wt_scales[0], [nc.sync] * 4)
         token_list = load_list("token_list", offs)
         xt_word_table = sb_tile("xt_word_table", [P, T], U32)
@@ -87,28 +87,23 @@ def tile_picked_tokens_store_one_doublepost_one_plain_kernel(
 
         wt_word = sb_tile("wt_word", [P, R], U16)
         nc.vector.tensor_copy(wt_word[:], wt_word_table[:].indirect(feature_list[:]))
-        wt_scale = sb_tile("wt_scale", [P, R], U8)
-        nc.vector.tensor_copy(wt_scale[:], wt_scale_table[:].indirect(feature_list[:]))
-        xt_word = picked.tile([P, J], U32, name="xt_word", offset=J + 2 * P, align_bytes=64)
+        wt_scale = sb_tile("wt_scale", [P, PACK, P], U8)
+        nc.vector.tensor_copy(wt_scale[:].rearrange("p t m -> p m t"), wt_scale_table[:].indirect(feature_list[:]))
+        xt_word = sb_tile("xt_word", [P, J], U32)
         nc.vector.tensor_copy(xt_word[:], xt_word_table[:].indirect(token_list[:]))
 
         word_by_t = wt_word[:].rearrange("p (m t) -> p t m", t=PACK)
-        scale_by_t = wt_scale[:].rearrange("p (m t) -> p t m", t=PACK)
         dealt_word = [None] * PACK
-        dealt_scale = [None] * PACK
 
-        def deal(t0, t1, words, scales):
+        def deal(t0, t1, words):
             nc.vector.tensor_copy(words[:], word_by_t[:, t0:t1])
-            nc.vector.tensor_copy(scales[:], scale_by_t[:, t0:t1])
             for t in range(t0, t1):
                 dealt_word[t] = words[:, t - t0].bitcast(FP4X4)
-                dealt_scale[t] = scales[:, t - t0]
 
-        xt_scale = picked.tile([P, J], U8, name="xt_scale", offset=0, align_bytes=64)
+        xt_scale = sb_tile("xt_scale", [P, J], U8)
         deal(
             0, 1,
             picked.tile([P, 1, P], U16, name="first_words", offset=J, align_bytes=64),
-            sb_tile("first_scales", [P, 1, P], U8),
         )
         for j0, j1 in SLOT_PIECES:
             tokens = token_list[:, j0 // 16 : j1 // 16]
@@ -117,7 +112,7 @@ def tile_picked_tokens_store_one_doublepost_one_plain_kernel(
         def first_product(t, j0, j1, bank):
             acc = psum.tile([P, j1 - j0], F32, name="acc_a%d_%d" % (t, j0), tag="bank%d" % bank)
             nc.tensor.matmul_mx(
-                out=acc[:], lhsT=dealt_word[t], lhsT_scale=dealt_scale[t],
+                out=acc[:], lhsT=dealt_word[t], lhsT_scale=wt_scale[:, t],
                 rhs=xt_word[:, j0:j1].bitcast(FP8X4), rhs_scale=xt_scale[:, j0:j1], start=True, stop=True,
             )
             return acc
@@ -128,7 +123,6 @@ def tile_picked_tokens_store_one_doublepost_one_plain_kernel(
         deal(
             1, PACK,
             reuse.tile([P, PACK - 1, P], U16, name="later_words", offset=0, align_bytes=64),
-            reuse.tile([P, PACK - 1, P], U8, name="later_scales", offset=2 * (PACK - 1) * P, align_bytes=64),
         )
         for t in range(1, PACK):
             nc.vector.tensor_copy(hidden[t][:], first_product(t, 0, J, 3 + t)[:])

from contextlib import ExitStack

import concourse.mybir as mybir

K, J, R, T, F, O, S, C, N = 512, 512, 512, 1024, 1024, 256, 256, 512, 256
FLOPS = 2 * K * R * J + 2 * R * N * O

F32 = mybir.dt.float32
BF16 = mybir.dt.bfloat16
I32 = mybir.dt.int32
U32 = mybir.dt.uint32
U16 = mybir.dt.uint16
U8 = mybir.dt.uint8
FP8X4 = mybir.dt.float8_e4m3fn_x4
FP4X4 = mybir.dt.float4_e2m1fn_x4
ALU = mybir.AluOpType
COPY = mybir.ActivationFunctionType.Copy

P = 128
PACK = 4
HALF = O // 2
SLOT_PIECES = ((0, 128), (128, 256), (256, 384), (384, 512))


def load_scale_rows(nc, plane, rows, queues):
    for q, queue in enumerate(queues):
        queue.dma_start(out=plane[32 * q : 32 * q + 4, :].bitcast(I32), in_=rows[4 * q : 4 * q + 4, :].bitcast(I32))


def tile_picked_tokens_store_one_doublepost_one_plain_kernel(
    tc, xt_words, xt_scales, wt_words, wt_scales, sa, sb, sd, wb_words, wb_scales,
    offs, offs2, offs3, offs4, offs5, offs6, offs7, out,
):
    nc = tc.nc
    with ExitStack() as ctx:
        keep = ctx.enter_context(tc.tile_pool(name="keep", bufs=1))
        reuse = ctx.enter_context(tc.tile_pool(name="reuse", bufs=1))
        seats = ctx.enter_context(tc.tile_pool(name="seats", bufs=1))
        picked = ctx.enter_context(tc.tile_pool(name="picked", bufs=1))
        psum = ctx.enter_context(tc.psum_pool(name="psum", bufs=1))

        def sb_tile(name, shape, dtype, tag=None):
            return keep.tile(shape, dtype, name=name, tag=tag or name, align_bytes=64)

        def load_list(name, src):
            lst = keep.tile(list(src.shape), U16, name=name)
            nc.sync.dma_start(lst[:], src)
            return lst

        def load_row_weights(name, src):
            w = keep.tile([P, PACK], F32, name=name)
            nc.sync.dma_start(out=w[:], in_=src.rearrange("(p t) one -> p (t one)", t=PACK))
            return w

        wt_scale_table = picked.tile([P, F], U8, name="wt_scale_table", offset=0, align_bytes=64)
        xt_scale_table = reuse.tile([P, T], U8, name="xt_scale_table", offset=0, align_bytes=64)
        wb_scale = sb_tile("wb_scale", [P, N], U8)
        for plane in (wt_scale_table, xt_scale_table, wb_scale):
            nc.vector.memset(plane[:].bitcast(I32), 0)
        boards_w = [sb_tile("board_w%d" % i, [P, C], F32) for i in range(2)]
        boards_v = [sb_tile("board_v%d" % i, [P, C], F32) for i in range(2)]
        for i in range(2):
            nc.vector.memset(boards_w[i][:], 0.0)
            nc.vector.memset(boards_v[i][:], 0.0)

        wt_word_table = sb_tile("wt_word_table", [P, F], U16)
        nc.sync.dma_start(out=wt_word_table[:].bitcast(I32), in_=wt_words[0].bitcast(I32))
        feature_list = load_list("feature_list", offs2)
        load_scale_rows(nc, wt_scale_table, wt_scales[0], [nc.sync] * 4)
        token_list = load_list("token_list", offs)
        xt_word_table = sb_tile("xt_word_table", [P, T], U32)
        nc.sync.dma_start(
            out=xt_word_table[:].bitcast(I32), in_=xt_words[0].rearrange("p n t -> p (n t)").bitcast(I32)
        )
        load_scale_rows(nc, xt_scale_table, xt_scales[0], [nc.sync] * 4)
        first_slots = load_list("first_slots", offs3)
        first_w = load_row_weights("first_w", sa)
        second_slots = load_list("second_slots", offs4)
        second_w = load_row_weights("second_w", sb)
        first_cols = load_list("first_cols", offs5)
        second_cols = load_list("second_cols", offs6)
        place_cols = load_list("place_cols", offs7)
        read_w = load_row_weights("read_w", sd)
        wb_word = sb_tile("wb_word", [P, N], U32)
        nc.sync.dma_start(out=wb_word[:].bitcast(I32), in_=wb_words[0].rearrange("p n t -> p (n t)").bitcast(I32))
        load_scale_rows(nc, wb_scale, wb_scales[0], [nc.sync] * 4)

        wt_word = sb_tile("wt_word", [P, R], U16)
        nc.vector.tensor_copy(wt_word[:], wt_word_table[:].indirect(feature_list[:]))
        wt_scale = sb_tile("wt_scale", [P, PACK, P], U8)
        nc.vector.tensor_copy(wt_scale[:].rearrange("p t m -> p m t"), wt_scale_table[:].indirect(feature_list[:]))
        xt_word = sb_tile("xt_word", [P, J], U32)
        nc.vector.tensor_copy(xt_word[:], xt_word_table[:].indirect(token_list[:]))

        word_by_t = wt_word[:].rearrange("p (m t) -> p t m", t=PACK)
        dealt_word = [None] * PACK

        def deal(t0, t1, words):
            nc.vector.tensor_copy(words[:], word_by_t[:, t0:t1])
            for t in range(t0, t1):
                dealt_word[t] = words[:, t - t0].bitcast(FP4X4)

        xt_scale = sb_tile("xt_scale", [P, J], U8)
        deal(
            0, 1,
            picked.tile([P, 1, P], U16, name="first_words", offset=J, align_bytes=64),
        )
        for j0, j1 in SLOT_PIECES:
            tokens = token_list[:, j0 // 16 : j1 // 16]
            nc.vector.tensor_copy(xt_scale[:, j0:j1], xt_scale_table[:].indirect(tokens))

        def first_product(t, j0, j1, bank):
            acc = psum.tile([P, j1 - j0], F32, name="acc_a%d_%d" % (t, j0), tag="bank%d" % bank)
            nc.tensor.matmul_mx(
                out=acc[:], lhsT=dealt_word[t], lhsT_scale=wt_scale[:, t],
                rhs=xt_word[:, j0:j1].bitcast(FP8X4), rhs_scale=xt_scale[:, j0:j1], start=True, stop=True,
            )
            return acc

        hidden = [sb_tile("hidden%d" % t, [P, J], F32) for t in range(PACK)]
        for i, (j0, j1) in enumerate(SLOT_PIECES):
            nc.scalar.activation(hidden[0][:, j0:j1], first_product(0, j0, j1, i)[:], COPY)
        deal(
            1, PACK,
            reuse.tile([P, PACK - 1, P], U16, name="later_words", offset=0, align_bytes=64),
        )
        for t in range(1, PACK):
            nc.vector.tensor_copy(hidden[t][:], first_product(t, 0, J, 3 + t)[:])

        gaps = []
        for t in range(PACK):
            h1 = sb_tile("h1_%d" % t, [P, S], F32, tag="h1")
            h2 = seats.tile([P, S], F32, name="h2_%d" % t, offset=512, align_bytes=64)
            nc.scalar.activation(h1[:], hidden[t][:].indirect(first_slots[:]), COPY, scale=first_w[:, t : t + 1])
            nc.scalar.activation(h2[:], hidden[t][:].indirect(second_slots[:]), COPY, scale=second_w[:, t : t + 1])
            board_w, board_v = boards_w[t % 2], boards_v[t % 2]
            nc.scalar.activation(board_w[:].indirect(first_cols[:]), h1[:], COPY)
            nc.scalar.activation(board_v[:].indirect(second_cols[:]), h2[:], COPY)
            diffs = [sb_tile("diff%d_%d" % (t, i), [P, C // 2], F32)[:] for i in range(2)]
            if t == PACK - 1:
                late_planes = seats.tile([P, PACK * C], BF16, name="late_planes", offset=1024, align_bytes=64)
                diffs[1] = late_planes[:, 2 * C : 3 * C].bitcast(F32)
            gap = sb_tile("gap%d" % t, [P, C], F32)
            halves = (slice(0, C // 2), slice(C // 2, C))
            for diff, cols in zip(diffs, halves):
                nc.vector.tensor_tensor(diff, board_w[:, cols], board_v[:, cols], ALU.subtract)
            for diff, cols in zip(diffs, halves):
                nc.vector.scalar_tensor_tensor(gap[:, cols], diff, -1.0, diff, ALU.mult, ALU.max)
            gaps.append(gap)

        early_planes = seats.tile([P, PACK, HALF], BF16, name="early_planes", offset=0, align_bytes=64)
        planes = [early_planes[:], late_planes[:].rearrange("p (t x) -> p t x", t=PACK)[:, :, 0:HALF]]
        for u in range(2):
            cols = place_cols[:, u * HALF // 16 : (u + 1) * HALF // 16]
            for t in range(PACK):
                nc.scalar.activation(planes[u][:, t], gaps[t][:].indirect(cols), COPY, scale=read_w[:, t : t + 1])

        codes = [sb_tile("codes%d" % u, [P, HALF], U32) for u in range(2)]
        scales = [sb_tile("scales%d" % u, [P, HALF], U8) for u in range(2)]
        for u, pieces in enumerate((((0, HALF),), ((0, HALF // 2), (HALF // 2, HALF)))):
            woven = [sb_tile("woven%d_%d" % (u, o0), [P, o1 - o0, PACK], BF16) for o0, o1 in pieces]
            for tile, (o0, o1) in zip(woven, pieces):
                nc.vector.tensor_copy(
                    tile[:].rearrange("p (c i) t -> p c t i", i=4),
                    planes[u][:, :, o0:o1].rearrange("p t (c i) -> p c t i", i=4),
                )
            for tile, (o0, o1) in zip(woven, pieces):
                nc.vector.quantize_mx(
                    out=codes[u][:, o0:o1].bitcast(FP8X4), scales=scales[u][:, o0:o1],
                    in_=tile[:].rearrange("p o t -> p (o t)"),
                )

        def second_product(acc, u, b):
            nc.tensor.matmul_mx(
                out=acc, lhsT=wb_word[:, b * P : (b + 1) * P].bitcast(FP8X4), lhsT_scale=wb_scale[:, b * P : (b + 1) * P],
                rhs=codes[u][:].bitcast(FP8X4), rhs_scale=scales[u][:], start=True, stop=True,
            )

        out_rows = out.rearrange("(b p) o -> p b o", p=P)
        acc0 = psum.tile([P, 2, HALF], F32, name="acc_out0", tag="bank0")
        for b in range(2):
            second_product(acc0[:, b], 0, b)
        result0 = sb_tile("result0", [P, 2, HALF], F32)
        nc.scalar.activation(result0[:], acc0[:], COPY)
        nc.sync.dma_start(out=out_rows[:, :, 0:HALF], in_=result0[:])
        for b in range(2):
            acc = psum.tile([P, HALF], F32, name="acc_out1_%d" % b, tag="bank%d" % (1 + b))
            second_product(acc[:], 1, b)
            result = sb_tile("result1_%d" % b, [P, HALF], F32)
            if b == 0:
                nc.vector.tensor_copy(result[:], acc[:])
                nc.sync.dma_start(out=out_rows[:, b, HALF:O], in_=result[:])
            else:
                nc.scalar.activation(result[:], acc[:], COPY)
                nc.scalar.dma_start(out=out_rows[:, b, HALF:O], in_=result[:])
